import numpy as np
import ml_dtypes


def mxq(x, axis, fmt="e4m3"):
    dtype, down = {"e4m3": (ml_dtypes.float8_e4m3fn, 7), "e5m2": (ml_dtypes.float8_e5m2, 14)}[fmt]
    v = np.moveaxis(np.asarray(x, np.float32).astype(ml_dtypes.bfloat16).astype(np.float64), axis, -1)
    blocks = v.reshape(v.shape[:-1] + (-1, 32))
    amax = np.abs(blocks).max(-1, keepdims=True)
    byte = np.maximum(np.where(amax > 0, np.frexp(amax)[1] - 1 + 127, 0) - down, 1)
    scale = np.exp2(byte - 127.0)
    codes = (blocks / scale).astype(np.float32).astype(dtype).astype(np.float64)
    return np.moveaxis((codes * scale).reshape(v.shape), -1, axis)


WIDE = False


def mx_kscale(k):
    if not WIDE:
        return np.ones(k)
    levels = np.array([10, -10, 5, -5, 0])
    if k % 512:
        return np.exp2(np.random.permutation(np.resize(levels, k // 32))).repeat(32)
    a = np.empty((k // 512, 16))
    for p in range(k // 512):
        a[p, :8] = np.random.permutation(np.resize(levels, 8))
        for g in range(8):
            far = levels[np.abs(levels - a[p, g]) >= 10]
            a[p, g + 8] = far[np.random.randint(len(far))]
    return np.exp2(a.ravel()).repeat(32)


def f64(x):
    return np.asarray(x).astype(np.float64)


def striped(idx):
    return np.tile(idx.reshape(-1, 16).T, (8, 1)).astype(np.uint16)


def unstriped(offs):
    return offs[:16].T.reshape(-1).astype(np.int64)


def pack_weight(w):
    k, n = w.shape
    w = f64(np.asarray(w, np.float32).astype(ml_dtypes.bfloat16)).reshape(k // 32, 32, n)
    amax = np.abs(w).max(1)
    byte = np.clip(np.where(amax > 0, np.frexp(amax)[1] - 1 + 127 - 7, 1), 1, 254)
    scaled = (w * np.exp2(127.0 - byte)[:, None, :]).reshape(k, n).astype(np.float32)
    words = np.ascontiguousarray(scaled.reshape(k // 512, 128, 4, n).transpose(0, 1, 3, 2)).astype(ml_dtypes.float8_e4m3fn).view(np.uint8)
    return words, np.ascontiguousarray(byte.astype(np.uint8).reshape(k // 512, 16, n))


def unpack_weight(words, scales):
    g, p, n, _ = words.shape
    vals = np.ascontiguousarray(words).view(ml_dtypes.float8_e4m3fn).astype(np.float64) * np.repeat(np.exp2(scales.astype(np.float64) - 127.0), 8, axis=1)[..., None]
    return vals.transpose(0, 1, 3, 2).reshape(g * 512, n)


E2M1 = np.array([0.0, 0.5, 1.0, 1.5, 2.0, 3.0, 4.0, 6.0, -0.0, -0.5, -1.0, -1.5, -2.0, -3.0, -4.0, -6.0])


def pack_fp4(w):
    k, n = w.shape
    w = f64(np.asarray(w, np.float32).astype(ml_dtypes.bfloat16)).reshape(k // 32, 32, n)
    amax = np.abs(w).max(1)
    mant, ex = np.frexp(amax / 6.0)
    byte = np.clip(np.where(amax > 0, np.where(mant > 0.5, ex, ex - 1) + 127, 1), 1, 254)
    scaled = (w * np.exp2(127.0 - byte)[:, None, :]).reshape(k, n).astype(np.float32)
    c = np.ascontiguousarray(scaled.reshape(k // 512, 128, 4, n).transpose(0, 1, 3, 2)).astype(ml_dtypes.float4_e2m1fn).view(np.uint8) & 0xF
    words = (c[..., 0::2] | (c[..., 1::2] << 4)).reshape(k // 512, 128, 2 * n)
    return np.ascontiguousarray(words), np.ascontiguousarray(byte.astype(np.uint8).reshape(k // 512, 16, n))


def unpack_fp4(words, scales):
    g, _, n = scales.shape
    words = np.ascontiguousarray(words).reshape(g, 128, n, 2)
    nib = np.empty((g, 128, n, 4), np.uint8)
    nib[..., 0::2] = words & 0xF
    nib[..., 1::2] = words >> 4
    vals = E2M1[nib] * np.repeat(np.exp2(scales.astype(np.float64) - 127.0), 8, axis=1)[..., None]
    return vals.transpose(0, 1, 3, 2).reshape(g * 512, n)


def planes(y):
    n, m = y.shape
    v = y.astype(np.float32).astype(ml_dtypes.bfloat16).astype(np.float64).reshape(n // 32, 32, m)
    top = np.abs(v).max(1)
    byte = np.clip(np.where(top > 0, np.frexp(top)[1] - 1 + 127 - 7, 1), 1, 254)
    codes = (v * np.exp2(127.0 - byte)[:, None, :]).reshape(n, m).astype(np.float32).astype(ml_dtypes.float8_e4m3fn).view(np.uint8)
    words = codes.reshape(n // 512, 128, 4, m).transpose(0, 1, 3, 2)
    return np.ascontiguousarray(words), np.ascontiguousarray(byte.astype(np.uint8).reshape(n // 512, 16, m))


K, T, S, N, H, W = 512, 2048, 512, 512, 512, 2048


def setup_inputs():
    n = np.random.standard_normal
    s = mx_kscale(K)[:, None]
    u = mx_kscale(S)
    packed_xT = pack_weight(n((K, T)) * s)
    packed_w1 = pack_fp4(n((S, N)) / np.sqrt(S) / u[:, None])
    return {
        "x_words": packed_xT[0],
        "x_scales": packed_xT[1],
        "wa": (n((K, H)) / np.sqrt(K) / s).astype(np.float32),
        "wb": (n((K, H)) / np.sqrt(K) / s).astype(np.float32),
        "tau": np.random.uniform(0.3, 0.9, (S, 1)).astype(np.float32),
        "gt": (np.random.uniform(0.5, 1.5, (S, 1)) * u[:, None]).astype(np.float32),
        "w1_words": packed_w1[0],
        "w1_scales": packed_w1[1],
        "tau2": np.random.uniform(0.3, 0.9, (N, 1)).astype(np.float32),
        "offs": striped(np.random.permutation(T)[:S]),
        "two": striped(np.random.permutation(T)[:S]),
        "n1": striped(np.random.permutation(H)),
        "n2": striped(np.random.permutation(H)),
        "n3": striped(np.random.randint(0, H, W)),
    }


def reference(x_words, x_scales, wa, wb, tau, gt, w1_words, w1_scales, tau2, offs, two, n1, n2, n3):
    x_two = unpack_weight(x_words, x_scales)[:, unstriped(two)]
    d = x_two.T @ mxq(f64(wb), 0, "e4m3")
    top = d.max(axis=1, keepdims=True)
    ea = np.exp(f64(tau) * (d[:, unstriped(n1)] - top))
    xq = unpack_weight(x_words, x_scales)[:, unstriped(offs)]
    y = xq.T @ mxq(f64(wa), 0, "e4m3")
    z = f64(gt) * ((2.0 * ea) * (y - y[:, unstriped(n2)]) - (0.5 * d))
    h = unpack_fp4(w1_words, w1_scales).T @ mxq(z, 0, "e4m3")
    top2 = h.max(axis=1, keepdims=True)
    ea2 = np.exp(f64(tau2) * (h[:, unstriped(n3)] - top2))
    ms = ea2.reshape(N, H, 4).sum(axis=2)
    out_0 = np.log(ms + 0.25) - (0.5 * h)
    return (out_0,) + planes(out_0)

@@ -1,0 +1,332 @@
+from contextlib import ExitStack
+
+import concourse.mybir as mybir
+
+K, T, S, N, H, W = 512, 2048, 512, 512, 512, 2048
+FLOPS = 2 * (K * S * H + K * S * H + S * N * H)
+
+F32 = mybir.dt.float32
+BF16 = mybir.dt.bfloat16
+I32 = mybir.dt.int32
+U32 = mybir.dt.uint32
+U16 = mybir.dt.uint16
+U8 = mybir.dt.uint8
+FP8X4 = mybir.dt.float8_e4m3fn_x4
+FP4X4 = mybir.dt.float4_e2m1fn_x4
+ALU = mybir.AluOpType
+ACT = mybir.ActivationFunctionType
+AX = mybir.AxisListType
+
+P = 128
+PACK = 4
+W_CHUNKS = [(0, 256), (256, 512)]
+Z_CHUNKS = [(0, 256), (256, 512)]
+MM_CHUNKS = [(0, 0, 256), (1, 256, 512)]
+Y_ON_VECTOR = (1, 3)
+O_CHUNKS = [(0, 128), (128, 256), (256, 384), (384, 512)]
+H_WINDOW = 2048
+H_PIECE = 1024
+
+
+def tile_picked_twtpxbegl_none_po_kernel(
+    tc, x_words, x_scales, wa, wb, tau, gt, w1_words, w1_scales, tau2, offs, two, n1, n2, n3, out_0, out_1, out_2
+):
+    nc = tc.nc
+    with ExitStack() as ctx:
+        keep = ctx.enter_context(tc.tile_pool(name="keep", bufs=1))
+        psum = ctx.enter_context(tc.psum_pool(name="psum", bufs=1))
+
+        def sb(name, shape, dtype):
+            return keep.tile(shape, dtype, name=name, align_bytes=64)
+
+        def bank(b):
+            return psum.tile([P, H], F32, name="bank", tag="bank%d" % b)
+
+        def load_list(name, src):
+            tile = keep.tile(list(src.shape), U16, name=name)
+            nc.sync.dma_start(tile[:], src)
+            return tile
+
+        def load_column(name, src, queue):
+            tile = sb(name, [P, PACK], F32)
+            queue.dma_start(out=tile[:], in_=src.rearrange("(p t) o -> p (t o)", t=PACK))
+            return tile
+
+        def load_scale_rows(queue, tile, src):
+            for q in range(4):
+                queue[q].dma_start(
+                    out=tile[32 * q : 32 * q + 4, :].bitcast(I32), in_=src[0, 4 * q : 4 * q + 4, :].bitcast(I32)
+                )
+
+        def load_weight(name, src, c0, c1):
+            tile = sb(name, [P, PACK, c1 - c0], F32)
+            nc.sync.dma_start(out=tile[:], in_=src[:, c0:c1].rearrange("(p j) c -> p j c", j=PACK))
+            return tile
+
+        xs = sb("xs", [P, T], U8)
+        nc.vector.memset(xs[:].bitcast(I32), 0)
+        two_t = load_list("two_t", two)
+        offs_t = load_list("offs_t", offs)
+        load_scale_rows([nc.sync, nc.sync, nc.scalar, nc.scalar], xs, x_scales)
+        w1w = sb("w1w", [P, 2 * N], U8)
+        nc.scalar.dma_start(out=w1w[:].bitcast(I32), in_=w1_words[0].bitcast(I32))
+        xw = sb("xw", [P, T], U32)
+        nc.sync.dma_start(out=xw[:].bitcast(I32), in_=x_words[0].rearrange("p c r -> p (c r)").bitcast(I32))
+        wb_raw = [load_weight("wb_raw%d" % i, wb, c0, c1) for i, (c0, c1) in enumerate(W_CHUNKS)]
+        wa_raw = [load_weight("wa_raw%d" % i, wa, c0, c1) for i, (c0, c1) in enumerate(W_CHUNKS)]
+        n1_t = load_list("n1_t", n1)
+        n2_t = load_list("n2_t", n2)
+        n3_t = load_list("n3_t", n3)
+        w1s = sb("w1s", [P, N], U8)
+        tau_t = load_column("tau_t", tau, nc.gpsimd)
+        gt_t = load_column("gt_t", gt, nc.gpsimd)
+        nc.vector.memset(w1s[:].bitcast(I32), 0)
+        load_scale_rows([nc.sync] * 4, w1s, w1_scales)
+        tau2_t = load_column("tau2_t", tau2, nc.sync)
+
+        h_sb = [sb("h_sb%d" % t, [P, H_WINDOW], F32) for t in range(PACK)]
+        d_sb = [sb("d_sb%d" % t, [P, H], F32) for t in range(PACK)]
+        quarter = sb("quarter", [P, 1], F32)
+        nc.gpsimd.memset(quarter[:], 0.25)
+
+        def pick(name, table, dtype, lst):
+            tile = sb(name, [P, PACK, P], dtype)
+            nc.vector.tensor_copy(out=tile[:].rearrange("p t m -> p m t"), in_=table[:].indirect(lst[:]))
+            return tile
+
+        def interleave_views(dst, src):
+            return (
+                dst[:].rearrange("p (c i) j -> p c j i", i=4),
+                src.rearrange("p j (c i) -> p c j i", i=4),
+            )
+
+        def cast_weight(name, raw):
+            grouped = sb(name, [P, raw.shape[2], PACK], BF16)
+            dst, src = interleave_views(grouped, raw[:])
+            nc.scalar.activation(out=dst, in_=src, func=ACT.Copy)
+            return grouped
+
+        def quantize(name, grouped):
+            width = grouped.shape[1]
+            codes = sb(name + "_codes", [P, width], U32)
+            scales = sb(name + "_scales", [P, width], U8)
+            nc.vector.quantize_mx(
+                out=codes[:].bitcast(FP8X4), scales=scales[:], in_=grouped[:].rearrange("p c j -> p (c j)")
+            )
+            return codes, scales
+
+        two_s = pick("two_s", xs, U8, two_t)
+        offs_s = pick("offs_s", xs, U8, offs_t)
+        two_w = pick("two_w", xw, U32, two_t)
+        offs_w = pick("offs_w", xw, U32, offs_t)
+        wb_q = [quantize("wb_q%d" % i, cast_weight("wb_g%d" % i, raw)) for i, raw in enumerate(wb_raw)]
+        wa_g = [cast_weight("wa_g%d" % i, raw) for i, raw in enumerate(wa_raw)]
+        wa_q = [quantize("wa_q%d" % i, g) for i, g in enumerate(wa_g)]
+
+        def project(words, scales, weight_q, first_bank):
+            banks = [bank(first_bank + t) for t in range(PACK)]
+            for t in range(PACK):
+                for (c0, c1), (codes, planes) in zip(W_CHUNKS, weight_q):
+                    nc.tensor.matmul_mx(
+                        out=banks[t][:, c0:c1],
+                        lhsT=words[:, t, :].bitcast(FP8X4),
+                        lhsT_scale=scales[:, t, :],
+                        rhs=codes[:].bitcast(FP8X4),
+                        rhs_scale=planes[:],
+                        start=True,
+                        stop=True,
+                    )
+            return banks
+
+        d_ps = project(two_w, two_s, wb_q, 0)
+        y_ps = project(offs_w, offs_s, wa_q, PACK)
+
+        g2 = sb("g2", [P, PACK], F32)
+        gh = sb("gh", [P, PACK], F32)
+        nc.gpsimd.tensor_scalar(out=g2[:], in0=gt_t[:], scalar1=2.0, scalar2=0.0, op0=ALU.mult, op1=ALU.add)
+        nc.gpsimd.tensor_scalar(out=gh[:], in0=gt_t[:], scalar1=-0.5, scalar2=0.0, op0=ALU.mult, op1=ALU.add)
+
+        top = sb("top", [P, PACK], F32)
+        bias = sb("bias", [P, PACK], F32)
+        y_sb = sb("y_sb", [P, PACK, H], F32)
+        half = H // 2
+        spare = [h_sb[k // 3][:, H * (1 + k % 3) : H * (2 + k % 3)] for k in range(3 * PACK)]
+        ea_late = h_sb[0][:, H : 3 * H]
+        ea = [
+            [spare[2 + t // 2][:, half * (t % 2) : half * (t % 2 + 1)] for t in range(PACK)],
+            [ea_late[:, half * t : half * (t + 1)] for t in range(PACK)],
+        ]
+        yg_slots = [ea_late[:, half // 2 + H * s : half // 2 + H * s + half] for s in range(2)]
+        u = spare[4:8]
+        v = spare[8:12]
+
+        w1w_d = sb("w1w_d", [P, PACK, P, 2], U8)
+        w1s_d = sb("w1s_d", [P, PACK, P], U8)
+        nc.scalar.copy(
+            out=w1w_d[:].rearrange("p t m b -> p t (m b)").bitcast(U16),
+            in_=w1w[:].bitcast(U16).rearrange("p (m t) -> p t m", t=PACK),
+        )
+
+        def leave_d(t):
+            col = slice(t, t + 1)
+            nc.vector.tensor_scalar(
+                out=d_sb[t][:], in0=d_ps[t][:], scalar1=1.0, scalar2=None, op0=ALU.mult, op1=ALU.max,
+                accum_out=top[:, col],
+            )
+            nc.gpsimd.tensor_scalar(
+                out=bias[:, col], in0=top[:, col], scalar1=tau_t[:, col], scalar2=-1.0, op0=ALU.mult, op1=ALU.mult
+            )
+
+        def leave_y(t):
+            col = slice(t, t + 1)
+            if t in Y_ON_VECTOR:
+                nc.vector.tensor_scalar(
+                    out=y_sb[:, t, :], in0=y_ps[t][:], scalar1=g2[:, col], scalar2=None, op0=ALU.mult
+                )
+            else:
+                nc.scalar.activation(out=y_sb[:, t, :], in_=y_ps[t][:], func=ACT.Copy, scale=g2[:, col])
+
+        zb = [sb("zb%d" % ci, [P, PACK, c1 - c0], BF16) for ci, (c0, c1) in enumerate(Z_CHUNKS)]
+
+        def exp_d(ci, t):
+            c0, c1 = Z_CHUNKS[ci]
+            col = slice(t, t + 1)
+            nc.scalar.activation(
+                out=ea[ci][t], in_=d_sb[t][:].indirect(n1_t[:, c0 // 16 : c1 // 16]), func=ACT.Exp,
+                bias=bias[:, col], scale=tau_t[:, col],
+            )
+
+        def diff_y(ci, t):
+            c0, c1 = Z_CHUNKS[ci]
+            yg = yg_slots[t % 2]
+            nc.scalar.activation(
+                out=yg, in_=y_sb[:, t, :].indirect(n2_t[:, c0 // 16 : c1 // 16]), func=ACT.Copy
+            )
+            nc.vector.tensor_tensor(out=u[t][:, c0:c1], in0=y_sb[:, t, c0:c1], in1=yg, op=ALU.subtract)
+
+        def mix(ci, t):
+            c0, c1 = Z_CHUNKS[ci]
+            nc.vector.tensor_tensor(out=v[t][:, c0:c1], in0=u[t][:, c0:c1], in1=ea[ci][t], op=ALU.mult)
+            nc.vector.scalar_tensor_tensor(
+                out=zb[ci][:, t, :], in0=d_sb[t][:, c0:c1], scalar=gh[:, t : t + 1], in1=v[t][:, c0:c1],
+                op0=ALU.mult, op1=ALU.add,
+            )
+
+        def quantize_z(ci):
+            c0, c1 = Z_CHUNKS[ci]
+            zi = sb("zi%d" % ci, [P, c1 - c0, PACK], BF16)
+            dst, src = interleave_views(zi, zb[ci][:])
+            nc.vector.tensor_copy(out=dst, in_=src)
+            return quantize("z_q%d" % ci, zi)
+
+        leave_d(0)
+        exp_d(0, 0)
+        leave_d(1)
+        exp_d(0, 1)
+        nc.gpsimd.tensor_copy(out=w1s_d[:], in_=w1s[:].rearrange("p (m t) -> p t m", t=PACK))
+        leave_y(0)
+        leave_y(1)
+        leave_d(2)
+        leave_d(3)
+        leave_y(3)
+        diff_y(0, 0)
+        diff_y(0, 1)
+        mix(0, 0)
+        leave_y(2)
+        exp_d(0, 2)
+        mix(0, 1)
+        diff_y(0, 2)
+        exp_d(0, 3)
+        diff_y(0, 3)
+        mix(0, 2)
+        diff_y(1, 0)
+        mix(0, 3)
+        diff_y(1, 1)
+        z_q = [quantize_z(0)]
+        diff_y(1, 2)
+        diff_y(1, 3)
+        for t in range(PACK):
+            exp_d(1, t)
+            mix(1, t)
+        z_q.append(quantize_z(1))
+
+        top2 = sb("top2", [P, PACK], F32)
+        bias2 = sb("bias2", [P, PACK], F32)
+        h_ps = [bank(PACK + t) for t in range(PACK)]
+        for ci, c0, c1 in MM_CHUNKS:
+            cols = slice(c0 - Z_CHUNKS[ci][0], c1 - Z_CHUNKS[ci][0])
+            codes, planes = z_q[ci]
+            for t in range(PACK):
+                nc.tensor.matmul_mx(
+                    out=h_ps[t][:, c0:c1],
+                    lhsT=w1w_d[:, t, :, :].rearrange("p m b -> p (m b)").bitcast(FP4X4),
+                    lhsT_scale=w1s_d[:, t, :],
+                    rhs=codes[:, cols].bitcast(FP8X4),
+                    rhs_scale=planes[:, cols],
+                    start=True,
+                    stop=True,
+                )
+        for t in range(PACK):
+            col = slice(t, t + 1)
+            nc.vector.tensor_scalar(
+                out=h_sb[t][:, 0:H], in0=h_ps[t][:], scalar1=1.0, scalar2=None, op0=ALU.mult, op1=ALU.max,
+                accum_out=top2[:, col],
+            )
+            nc.vector.tensor_scalar(
+                out=bias2[:, col], in0=top2[:, col], scalar1=tau2_t[:, col], scalar2=-1.0,
+                op0=ALU.mult, op1=ALU.mult,
+            )
+
+        ms = sb("ms", [P, PACK, H], F32)
+        hh = sb("hh", [P, PACK, H], F32)
+        for t in range(PACK):
+            col = slice(t, t + 1)
+            for e0 in range(0, W, H_PIECE):
+                e1 = e0 + H_PIECE
+                ea2 = keep.tile([P, H_PIECE], F32, name="ea2", tag="ea2", bufs=3, align_bytes=64)
+                nc.scalar.activation(
+                    out=ea2[:], in_=h_sb[t][:].indirect(n3_t[:, e0 // 16 : e1 // 16]), func=ACT.Exp,
+                    bias=bias2[:, col], scale=tau2_t[:, col],
+                )
+                nc.vector.tensor_reduce(
+                    out=ms[:, t, e0 // 4 : e1 // 4], in_=ea2[:].rearrange("p (j r) -> p j r", r=4), axis=AX.X,
+                    op=ALU.add,
+                )
+            nc.vector.tensor_scalar(
+                out=hh[:, t, :], in0=h_sb[t][:, 0:H], scalar1=-0.5, scalar2=None, op0=ALU.mult
+            )
+
+        out_rows = out_0.rearrange("(p t) j -> p t j", t=PACK)
+        out_words = out_1[0].rearrange("p c r -> p (c r)").bitcast(I32)
+        o_codes = sb("o_codes", [P, H], U32)
+        o_scales = sb("o_scales", [P, H], U8)
+        o_t, oi_t = [], []
+        for ci, (c0, c1) in enumerate(O_CHUNKS):
+            w = c1 - c0
+            lg = sb("lg%d" % ci, [P, PACK, w], F32)
+            o = sb("o%d" % ci, [P, PACK, w], F32)
+            nc.scalar.activation(out=lg[:], in_=ms[:, :, c0:c1], func=ACT.Ln, bias=quarter[:])
+            nc.vector.tensor_tensor(out=o[:], in0=lg[:], in1=hh[:, :, c0:c1], op=ALU.add)
+            nc.sync.dma_start(out=out_rows[:, :, c0:c1], in_=o[:])
+            o_t.append(o)
+        for ci in (2, 3, 0, 1):
+            c0, c1 = O_CHUNKS[ci]
+            oi = sb("oi%d" % ci, [P, c1 - c0, PACK], BF16)
+            dst, src = interleave_views(oi, o_t[ci][:])
+            if ci < 2:
+                nc.scalar.copy(out=dst, in_=src)
+            else:
+                nc.vector.tensor_copy(out=dst, in_=src)
+            oi_t.append((ci, oi))
+        for ci, oi in sorted(oi_t, key=lambda e: (0, 2, 1, 3)[e[0]]):
+            c0, c1 = O_CHUNKS[ci]
+            nc.vector.quantize_mx(
+                out=o_codes[:, c0:c1].bitcast(FP8X4), scales=o_scales[:, c0:c1],
+                in_=oi[:].rearrange("p c j -> p (c j)"),
+            )
+        nc.sync.dma_start(out=out_words, in_=o_codes[:].bitcast(I32))
+        for q in range(4):
+            queue = nc.scalar if q % 2 == 0 else nc.sync
+            queue.dma_start(
+                out=out_2[0, 4 * q : 4 * q + 4, :].bitcast(I32), in_=o_scales[32 * q : 32 * q + 4, :].bitcast(I32)
+            )

@@ -21,9 +21,9 @@ P = 128
 PACK = 4
 W_CHUNKS = [(0, 256), (256, 512)]
 Z_CHUNKS = [(0, 256), (256, 512)]
-MM_CHUNKS = [(0, 0, 256), (1, 256, 512)]
-Y_ON_VECTOR = (1, 3)
-O_CHUNKS = [(0, 128), (128, 256), (256, 384), (384, 512)]
+O_GROUPS = [[(0, 64), (64, 192)], [(192, 320)], [(320, 448), (448, 512)]]
+O_ON_SCALAR = (64, 192, 320)
+WORDS_SPLIT = 320
 H_WINDOW = 2048
 H_PIECE = 1024
 
@@ -37,7 +37,7 @@ def tile_picked_twtpxbegl_none_po_kernel(
         psum = ctx.enter_context(tc.psum_pool(name="psum", bufs=1))
 
         def sb(name, shape, dtype):
-            return keep.tile(shape, dtype, name=name, align_bytes=64)
+            return keep.tile(shape, dtype, name=name, tag=name, align_bytes=64)
 
         def bank(b):
             return psum.tile([P, H], F32, name="bank", tag="bank%d" % b)
@@ -65,27 +65,30 @@ def tile_picked_twtpxbegl_none_po_kernel(
 
         xs = sb("xs", [P, T], U8)
         nc.vector.memset(xs[:].bitcast(I32), 0)
-        two_t = load_list("two_t", two)
         offs_t = load_list("offs_t", offs)
+        two_t = load_list("two_t", two)
         load_scale_rows([nc.sync, nc.sync, nc.scalar, nc.scalar], xs, x_scales)
-        w1w = sb("w1w", [P, 2 * N], U8)
-        nc.scalar.dma_start(out=w1w[:].bitcast(I32), in_=w1_words[0].bitcast(I32))
         xw = sb("xw", [P, T], U32)
         nc.sync.dma_start(out=xw[:].bitcast(I32), in_=x_words[0].rearrange("p c r -> p (c r)").bitcast(I32))
-        wb_raw = [load_weight("wb_raw%d" % i, wb, c0, c1) for i, (c0, c1) in enumerate(W_CHUNKS)]
         wa_raw = [load_weight("wa_raw%d" % i, wa, c0, c1) for i, (c0, c1) in enumerate(W_CHUNKS)]
-        n1_t = load_list("n1_t", n1)
+        wb_raw = [load_weight("wb_raw%d" % i, wb, c0, c1) for i, (c0, c1) in enumerate(W_CHUNKS)]
         n2_t = load_list("n2_t", n2)
+        n1_t = load_list("n1_t", n1)
+        w1w = sb("w1w", [P, 2 * N], U8)
+        nc.sync.dma_start(out=w1w[:].bitcast(I32), in_=w1_words[0].bitcast(I32))
         n3_t = load_list("n3_t", n3)
         w1s = sb("w1s", [P, N], U8)
-        tau_t = load_column("tau_t", tau, nc.gpsimd)
         gt_t = load_column("gt_t", gt, nc.gpsimd)
+        tau_t = load_column("tau_t", tau, nc.gpsimd)
         nc.vector.memset(w1s[:].bitcast(I32), 0)
         load_scale_rows([nc.sync] * 4, w1s, w1_scales)
         tau2_t = load_column("tau2_t", tau2, nc.sync)
 
         h_sb = [sb("h_sb%d" % t, [P, H_WINDOW], F32) for t in range(PACK)]
-        d_sb = [sb("d_sb%d" % t, [P, H], F32) for t in range(PACK)]
+        d_sb = [sb("d_sb%d" % t, [P, 2 * H], F32) for t in range(PACK)]
+        y_sb = [sb("y_sb%d" % t, [P, H + 16], F32) for t in range(PACK)]
+        for t in range(PACK):
+            nc.vector.memset(y_sb[t][:, H:], 0.0)
         quarter = sb("quarter", [P, 1], F32)
         nc.gpsimd.memset(quarter[:], 0.25)
 
@@ -115,13 +118,12 @@ def tile_picked_twtpxbegl_none_po_kernel(
             )
             return codes, scales
 
-        two_s = pick("two_s", xs, U8, two_t)
         offs_s = pick("offs_s", xs, U8, offs_t)
-        two_w = pick("two_w", xw, U32, two_t)
+        two_s = pick("two_s", xs, U8, two_t)
         offs_w = pick("offs_w", xw, U32, offs_t)
+        two_w = pick("two_w", xw, U32, two_t)
+        wa_q = [quantize("wa_q%d" % i, cast_weight("wa_g%d" % i, raw)) for i, raw in enumerate(wa_raw)]
         wb_q = [quantize("wb_q%d" % i, cast_weight("wb_g%d" % i, raw)) for i, raw in enumerate(wb_raw)]
-        wa_g = [cast_weight("wa_g%d" % i, raw) for i, raw in enumerate(wa_raw)]
-        wa_q = [quantize("wa_q%d" % i, g) for i, g in enumerate(wa_g)]
 
         def project(words, scales, weight_q, first_bank):
             banks = [bank(first_bank + t) for t in range(PACK)]
@@ -138,144 +140,112 @@ def tile_picked_twtpxbegl_none_po_kernel(
                     )
             return banks
 
-        d_ps = project(two_w, two_s, wb_q, 0)
         y_ps = project(offs_w, offs_s, wa_q, PACK)
+        d_ps = project(two_w, two_s, wb_q, 0)
 
         g2 = sb("g2", [P, PACK], F32)
         gh = sb("gh", [P, PACK], F32)
         nc.gpsimd.tensor_scalar(out=g2[:], in0=gt_t[:], scalar1=2.0, scalar2=0.0, op0=ALU.mult, op1=ALU.add)
         nc.gpsimd.tensor_scalar(out=gh[:], in0=gt_t[:], scalar1=-0.5, scalar2=0.0, op0=ALU.mult, op1=ALU.add)
 
+        ntau2 = sb("ntau2", [P, PACK], F32)
+        nc.gpsimd.tensor_scalar(out=ntau2[:], in0=tau2_t[:], scalar1=-1.0, scalar2=0.0, op0=ALU.mult, op1=ALU.add)
         top = sb("top", [P, PACK], F32)
         bias = sb("bias", [P, PACK], F32)
-        y_sb = sb("y_sb", [P, PACK, H], F32)
-        half = H // 2
-        spare = [h_sb[k // 3][:, H * (1 + k % 3) : H * (2 + k % 3)] for k in range(3 * PACK)]
-        ea_late = h_sb[0][:, H : 3 * H]
-        ea = [
-            [spare[2 + t // 2][:, half * (t % 2) : half * (t % 2 + 1)] for t in range(PACK)],
-            [ea_late[:, half * t : half * (t + 1)] for t in range(PACK)],
-        ]
-        yg_slots = [ea_late[:, half // 2 + H * s : half // 2 + H * s + half] for s in range(2)]
-        u = spare[4:8]
-        v = spare[8:12]
+        ea = [h_sb[t][:, H : 2 * H] for t in range(PACK)]
+        u = [h_sb[t][:, 2 * H : 3 * H] for t in range(PACK)]
+        v = [h_sb[t][:, 3 * H : 4 * H] for t in range(PACK)]
+        yg = [d_sb[t][:, H : 2 * H] for t in range(PACK)]
+        zb = sb("zb", [P, PACK, H], BF16)
 
-        w1w_d = sb("w1w_d", [P, PACK, P, 2], U8)
-        w1s_d = sb("w1s_d", [P, PACK, P], U8)
-        nc.scalar.copy(
-            out=w1w_d[:].rearrange("p t m b -> p t (m b)").bitcast(U16),
-            in_=w1w[:].bitcast(U16).rearrange("p (m t) -> p t m", t=PACK),
-        )
-
-        def leave_d(t):
+        for t in range(PACK):
+            nc.vector.tensor_scalar(
+                out=y_sb[t][:, 0:H], in0=y_ps[t][:], scalar1=g2[:, t : t + 1], scalar2=None, op0=ALU.mult
+            )
+            nc.scalar.activation(out=yg[t], in_=y_sb[t][:].indirect(n2_t[:]), func=ACT.Copy)
+        for t in range(PACK):
             col = slice(t, t + 1)
             nc.vector.tensor_scalar(
-                out=d_sb[t][:], in0=d_ps[t][:], scalar1=1.0, scalar2=None, op0=ALU.mult, op1=ALU.max,
+                out=d_sb[t][:, 0:H], in0=d_ps[t][:], scalar1=1.0, scalar2=None, op0=ALU.mult, op1=ALU.max,
                 accum_out=top[:, col],
             )
             nc.gpsimd.tensor_scalar(
                 out=bias[:, col], in0=top[:, col], scalar1=tau_t[:, col], scalar2=-1.0, op0=ALU.mult, op1=ALU.mult
             )
+        w1s_d = sb("w1s_d", [P, PACK, P], U8)
+        nc.gpsimd.tensor_copy(out=w1s_d[:], in_=w1s[:].rearrange("p (m t) -> p t m", t=PACK))
+        for t in range(PACK):
+            nc.vector.tensor_tensor(out=u[t], in0=y_sb[t][:, 0:H], in1=yg[t], op=ALU.subtract)
 
-        def leave_y(t):
-            col = slice(t, t + 1)
-            if t in Y_ON_VECTOR:
-                nc.vector.tensor_scalar(
-                    out=y_sb[:, t, :], in0=y_ps[t][:], scalar1=g2[:, col], scalar2=None, op0=ALU.mult
-                )
-            else:
-                nc.scalar.activation(out=y_sb[:, t, :], in_=y_ps[t][:], func=ACT.Copy, scale=g2[:, col])
-
-        zb = [sb("zb%d" % ci, [P, PACK, c1 - c0], BF16) for ci, (c0, c1) in enumerate(Z_CHUNKS)]
-
-        def exp_d(ci, t):
-            c0, c1 = Z_CHUNKS[ci]
+        def exp_d(t, c0, c1):
             col = slice(t, t + 1)
             nc.scalar.activation(
-                out=ea[ci][t], in_=d_sb[t][:].indirect(n1_t[:, c0 // 16 : c1 // 16]), func=ACT.Exp,
+                out=ea[t][:, c0:c1], in_=d_sb[t][:].indirect(n1_t[:, c0 // 16 : c1 // 16]), func=ACT.Exp,
                 bias=bias[:, col], scale=tau_t[:, col],
             )
 
-        def diff_y(ci, t):
-            c0, c1 = Z_CHUNKS[ci]
-            yg = yg_slots[t % 2]
-            nc.scalar.activation(
-                out=yg, in_=y_sb[:, t, :].indirect(n2_t[:, c0 // 16 : c1 // 16]), func=ACT.Copy
-            )
-            nc.vector.tensor_tensor(out=u[t][:, c0:c1], in0=y_sb[:, t, c0:c1], in1=yg, op=ALU.subtract)
-
-        def mix(ci, t):
-            c0, c1 = Z_CHUNKS[ci]
-            nc.vector.tensor_tensor(out=v[t][:, c0:c1], in0=u[t][:, c0:c1], in1=ea[ci][t], op=ALU.mult)
+        def mix(t, c0, c1):
+            nc.vector.tensor_tensor(out=v[t][:, c0:c1], in0=u[t][:, c0:c1], in1=ea[t][:, c0:c1], op=ALU.mult)
             nc.vector.scalar_tensor_tensor(
-                out=zb[ci][:, t, :], in0=d_sb[t][:, c0:c1], scalar=gh[:, t : t + 1], in1=v[t][:, c0:c1],
+                out=zb[:, t, c0:c1], in0=d_sb[t][:, c0:c1], scalar=gh[:, t : t + 1], in1=v[t][:, c0:c1],
                 op0=ALU.mult, op1=ALU.add,
             )
 
-        def quantize_z(ci):
-            c0, c1 = Z_CHUNKS[ci]
-            zi = sb("zi%d" % ci, [P, c1 - c0, PACK], BF16)
-            dst, src = interleave_views(zi, zb[ci][:])
-            nc.vector.tensor_copy(out=dst, in_=src)
-            return quantize("z_q%d" % ci, zi)
-
-        leave_d(0)
-        exp_d(0, 0)
-        leave_d(1)
-        exp_d(0, 1)
-        nc.gpsimd.tensor_copy(out=w1s_d[:], in_=w1s[:].rearrange("p (m t) -> p t m", t=PACK))
-        leave_y(0)
-        leave_y(1)
-        leave_d(2)
-        leave_d(3)
-        leave_y(3)
-        diff_y(0, 0)
-        diff_y(0, 1)
-        mix(0, 0)
-        leave_y(2)
-        exp_d(0, 2)
-        mix(0, 1)
-        diff_y(0, 2)
-        exp_d(0, 3)
-        diff_y(0, 3)
-        mix(0, 2)
-        diff_y(1, 0)
-        mix(0, 3)
-        diff_y(1, 1)
-        z_q = [quantize_z(0)]
-        diff_y(1, 2)
-        diff_y(1, 3)
-        for t in range(PACK):
-            exp_d(1, t)
-            mix(1, t)
-        z_q.append(quantize_z(1))
+        for t in range(PACK - 1):
+            exp_d(t, 0, H)
+            mix(t, 0, H)
+        for c0, c1 in Z_CHUNKS:
+            exp_d(PACK - 1, c0, c1)
+        w1w_d = keep.tile([P, PACK, P, 2], U8, name="w1w_d", tag="y_sb3", align_bytes=64)
+        nc.scalar.copy(
+            out=w1w_d[:].rearrange("p t m b -> p t (m b)").bitcast(U16),
+            in_=w1w[:].bitcast(U16).rearrange("p (m t) -> p t m", t=PACK),
+        )
+        z_codes = sb("z_codes", [P, H], U32)
+        z_scales = sb("z_scales", [P, H], U8)
+        zi = []
+        for ci, (c0, c1) in enumerate(Z_CHUNKS):
+            mix(PACK - 1, c0, c1)
+            grouped = sb("zi%d" % ci, [P, c1 - c0, PACK], BF16)
+            dst, src = interleave_views(grouped, zb[:, :, c0:c1])
+            if ci == 0:
+                nc.scalar.copy(out=dst, in_=src)
+            else:
+                nc.vector.tensor_copy(out=dst, in_=src)
+            zi.append(grouped)
+        for (c0, c1), grouped in zip(Z_CHUNKS, zi):
+            nc.vector.quantize_mx(
+                out=z_codes[:, c0:c1].bitcast(FP8X4), scales=z_scales[:, c0:c1],
+                in_=grouped[:].rearrange("p c j -> p (c j)"),
+            )
 
         top2 = sb("top2", [P, PACK], F32)
-        bias2 = sb("bias2", [P, PACK], F32)
-        h_ps = [bank(PACK + t) for t in range(PACK)]
-        for ci, c0, c1 in MM_CHUNKS:
-            cols = slice(c0 - Z_CHUNKS[ci][0], c1 - Z_CHUNKS[ci][0])
-            codes, planes = z_q[ci]
-            for t in range(PACK):
-                nc.tensor.matmul_mx(
-                    out=h_ps[t][:, c0:c1],
-                    lhsT=w1w_d[:, t, :, :].rearrange("p m b -> p (m b)").bitcast(FP4X4),
-                    lhsT_scale=w1s_d[:, t, :],
-                    rhs=codes[:, cols].bitcast(FP8X4),
-                    rhs_scale=planes[:, cols],
-                    start=True,
-                    stop=True,
-                )
-        for t in range(PACK):
+        top2_part = sb("top2_part", [P, 1], F32)
+        bias2 = [sb("bias2_%d" % t, [P, 1], F32) for t in range(PACK)]
+
+        def mix_places(t, b, c0, c1, start_max, row_max):
+            h_ps = bank(b)
+            nc.tensor.matmul_mx(
+                out=h_ps[:, 0 : c1 - c0],
+                lhsT=w1w_d[:, t, :, :].rearrange("p m b -> p (m b)").bitcast(FP4X4),
+                lhsT_scale=w1s_d[:, t, :],
+                rhs=z_codes[:, c0:c1].bitcast(FP8X4),
+                rhs_scale=z_scales[:, c0:c1],
+                start=True,
+                stop=True,
+            )
+            nc.vector.tensor_scalar(
+                out=h_sb[t][:, c0:c1], in0=h_ps[:, 0 : c1 - c0], scalar1=1.0, scalar2=start_max, op0=ALU.mult,
+                op1=ALU.max, accum_out=row_max,
+            )
+
+        mix_places(0, 0, 0, H // 2, None, top2_part[:])
+        mix_places(0, PACK, H // 2, H, top2_part[:], top2[:, 0:1])
+        nc.scalar.activation(out=bias2[0][:], in_=top2[:, 0:1], func=ACT.Copy, scale=ntau2[:, 0:1])
+        for t in range(1, PACK):
             col = slice(t, t + 1)
-            nc.vector.tensor_scalar(
-                out=h_sb[t][:, 0:H], in0=h_ps[t][:], scalar1=1.0, scalar2=None, op0=ALU.mult, op1=ALU.max,
-                accum_out=top2[:, col],
-            )
-            nc.vector.tensor_scalar(
-                out=bias2[:, col], in0=top2[:, col], scalar1=tau2_t[:, col], scalar2=-1.0,
-                op0=ALU.mult, op1=ALU.mult,
-            )
+            mix_places(t, PACK + t, 0, H, None, top2[:, col])
+            nc.vector.tensor_tensor(out=bias2[t][:], in0=top2[:, col], in1=ntau2[:, col], op=ALU.mult)
 
         ms = sb("ms", [P, PACK, H], F32)
         hh = sb("hh", [P, PACK, H], F32)
@@ -286,7 +256,7 @@ def tile_picked_twtpxbegl_none_po_kernel(
                 ea2 = keep.tile([P, H_PIECE], F32, name="ea2", tag="ea2", bufs=3, align_bytes=64)
                 nc.scalar.activation(
                     out=ea2[:], in_=h_sb[t][:].indirect(n3_t[:, e0 // 16 : e1 // 16]), func=ACT.Exp,
-                    bias=bias2[:, col], scale=tau2_t[:, col],
+                    bias=bias2[t][:], scale=tau2_t[:, col],
                 )
                 nc.vector.tensor_reduce(
                     out=ms[:, t, e0 // 4 : e1 // 4], in_=ea2[:].rearrange("p (j r) -> p j r", r=4), axis=AX.X,
@@ -300,31 +270,30 @@ def tile_picked_twtpxbegl_none_po_kernel(
         out_words = out_1[0].rearrange("p c r -> p (c r)").bitcast(I32)
         o_codes = sb("o_codes", [P, H], U32)
         o_scales = sb("o_scales", [P, H], U8)
-        o_t, oi_t = [], []
-        for ci, (c0, c1) in enumerate(O_CHUNKS):
-            w = c1 - c0
-            lg = sb("lg%d" % ci, [P, PACK, w], F32)
-            o = sb("o%d" % ci, [P, PACK, w], F32)
-            nc.scalar.activation(out=lg[:], in_=ms[:, :, c0:c1], func=ACT.Ln, bias=quarter[:])
-            nc.vector.tensor_tensor(out=o[:], in0=lg[:], in1=hh[:, :, c0:c1], op=ALU.add)
-            nc.sync.dma_start(out=out_rows[:, :, c0:c1], in_=o[:])
-            o_t.append(o)
-        for ci in (2, 3, 0, 1):
-            c0, c1 = O_CHUNKS[ci]
-            oi = sb("oi%d" % ci, [P, c1 - c0, PACK], BF16)
-            dst, src = interleave_views(oi, o_t[ci][:])
-            if ci < 2:
+        rounding = []
+        for group in O_GROUPS:
+            g0, g1 = group[0][0], group[-1][1]
+            o = sb("o%d" % g0, [P, PACK, g1 - g0], F32)
+            for c0, c1 in group:
+                lg = sb("lg%d" % c0, [P, PACK, c1 - c0], F32)
+                nc.scalar.activation(out=lg[:], in_=ms[:, :, c0:c1], func=ACT.Ln, bias=quarter[:])
+                nc.vector.tensor_tensor(out=o[:, :, c0 - g0 : c1 - g0], in0=lg[:], in1=hh[:, :, c0:c1], op=ALU.add)
+                rounding.append((c0, c1, o[:, :, c0 - g0 : c1 - g0]))
+            nc.sync.dma_start(out=out_rows[:, :, g0:g1], in_=o[:])
+        for c0, c1, values in rounding:
+            oi = sb("oi%d" % c0, [P, c1 - c0, PACK], BF16)
+            dst, src = interleave_views(oi, values)
+            if c0 in O_ON_SCALAR:
                 nc.scalar.copy(out=dst, in_=src)
             else:
                 nc.vector.tensor_copy(out=dst, in_=src)
-            oi_t.append((ci, oi))
-        for ci, oi in sorted(oi_t, key=lambda e: (0, 2, 1, 3)[e[0]]):
-            c0, c1 = O_CHUNKS[ci]
             nc.vector.quantize_mx(
                 out=o_codes[:, c0:c1].bitcast(FP8X4), scales=o_scales[:, c0:c1],
                 in_=oi[:].rearrange("p c j -> p (c j)"),
             )
-        nc.sync.dma_start(out=out_words, in_=o_codes[:].bitcast(I32))
+            if c1 == WORDS_SPLIT:
+                nc.sync.dma_start(out=out_words[:, 0:c1], in_=o_codes[:, 0:c1].bitcast(I32))
+        nc.sync.dma_start(out=out_words[:, WORDS_SPLIT:], in_=o_codes[:, WORDS_SPLIT:].bitcast(I32))
         for q in range(4):
             queue = nc.scalar if q % 2 == 0 else nc.sync
             queue.dma_start(

from contextlib import ExitStack

import concourse.mybir as mybir

K, T, S, N, H, W = 512, 2048, 512, 512, 512, 2048
FLOPS = 2 * (K * S * H + K * S * H + S * N * H)

F32 = mybir.dt.float32
BF16 = mybir.dt.bfloat16
I32 = mybir.dt.int32
U32 = mybir.dt.uint32
U16 = mybir.dt.uint16
U8 = mybir.dt.uint8
FP8X4 = mybir.dt.float8_e4m3fn_x4
FP4X4 = mybir.dt.float4_e2m1fn_x4
ALU = mybir.AluOpType
ACT = mybir.ActivationFunctionType
AX = mybir.AxisListType

P = 128
PACK = 4
W_CHUNKS = [(0, 256), (256, 512)]
Z_CHUNKS = [(0, 256), (256, 512)]
O_GROUPS = [[(0, 64), (64, 192)], [(192, 320)], [(320, 448), (448, 512)]]
O_ON_SCALAR = (64, 192, 320)
WORDS_SPLIT = 320
H_WINDOW = 2048
H_PIECE = 1024


def tile_picked_twtpxbegl_none_po_kernel(
    tc, x_words, x_scales, wa, wb, tau, gt, w1_words, w1_scales, tau2, offs, two, n1, n2, n3, out_0, out_1, out_2
):
    nc = tc.nc
    with ExitStack() as ctx:
        keep = ctx.enter_context(tc.tile_pool(name="keep", bufs=1))
        psum = ctx.enter_context(tc.psum_pool(name="psum", bufs=1))

        def sb(name, shape, dtype):
            return keep.tile(shape, dtype, name=name, tag=name, align_bytes=64)

        def bank(b):
            return psum.tile([P, H], F32, name="bank", tag="bank%d" % b)

        def load_list(name, src):
            tile = keep.tile(list(src.shape), U16, name=name)
            nc.sync.dma_start(tile[:], src)
            return tile

        def load_column(name, src, queue):
            tile = sb(name, [P, PACK], F32)
            queue.dma_start(out=tile[:], in_=src.rearrange("(p t) o -> p (t o)", t=PACK))
            return tile

        def load_scale_rows(queue, tile, src):
            for q in range(4):
                queue[q].dma_start(
                    out=tile[32 * q : 32 * q + 4, :].bitcast(I32), in_=src[0, 4 * q : 4 * q + 4, :].bitcast(I32)
                )

        def load_weight(name, src, c0, c1):
            tile = sb(name, [P, PACK, c1 - c0], F32)
            nc.sync.dma_start(out=tile[:], in_=src[:, c0:c1].rearrange("(p j) c -> p j c", j=PACK))
            return tile

        xs = sb("xs", [P, T], U8)
        nc.vector.memset(xs[:].bitcast(I32), 0)
        offs_t = load_list("offs_t", offs)
        two_t = load_list("two_t", two)
        load_scale_rows([nc.sync, nc.sync, nc.scalar, nc.scalar], xs, x_scales)
        xw = sb("xw", [P, T], U32)
        nc.sync.dma_start(out=xw[:].bitcast(I32), in_=x_words[0].rearrange("p c r -> p (c r)").bitcast(I32))
        wa_raw = [load_weight("wa_raw%d" % i, wa, c0, c1) for i, (c0, c1) in enumerate(W_CHUNKS)]
        wb_raw = [load_weight("wb_raw%d" % i, wb, c0, c1) for i, (c0, c1) in enumerate(W_CHUNKS)]
        n2_t = load_list("n2_t", n2)
        n1_t = load_list("n1_t", n1)
        w1w = sb("w1w", [P, 2 * N], U8)
        nc.sync.dma_start(out=w1w[:].bitcast(I32), in_=w1_words[0].bitcast(I32))
        n3_t = load_list("n3_t", n3)
        w1s = sb("w1s", [P, N], U8)
        gt_t = load_column("gt_t", gt, nc.gpsimd)
        tau_t = load_column("tau_t", tau, nc.gpsimd)
        nc.vector.memset(w1s[:].bitcast(I32), 0)
        load_scale_rows([nc.sync] * 4, w1s, w1_scales)
        tau2_t = load_column("tau2_t", tau2, nc.sync)

        h_sb = [sb("h_sb%d" % t, [P, H_WINDOW], F32) for t in range(PACK)]
        d_sb = [sb("d_sb%d" % t, [P, 2 * H], F32) for t in range(PACK)]
        y_sb = [sb("y_sb%d" % t, [P, H + 16], F32) for t in range(PACK)]
        for t in range(PACK):
            nc.vector.memset(y_sb[t][:, H:], 0.0)
        quarter = sb("quarter", [P, 1], F32)
        nc.gpsimd.memset(quarter[:], 0.25)

        def pick(name, table, dtype, lst):
            tile = sb(name, [P, PACK, P], dtype)
            nc.vector.tensor_copy(out=tile[:].rearrange("p t m -> p m t"), in_=table[:].indirect(lst[:]))
            return tile

        def interleave_views(dst, src):
            return (
                dst[:].rearrange("p (c i) j -> p c j i", i=4),
                src.rearrange("p j (c i) -> p c j i", i=4),
            )

        def cast_weight(name, raw):
            grouped = sb(name, [P, raw.shape[2], PACK], BF16)
            dst, src = interleave_views(grouped, raw[:])
            nc.scalar.activation(out=dst, in_=src, func=ACT.Copy)
            return grouped

        def quantize(name, grouped):
            width = grouped.shape[1]
            codes = sb(name + "_codes", [P, width], U32)
            scales = sb(name + "_scales", [P, width], U8)
            nc.vector.quantize_mx(
                out=codes[:].bitcast(FP8X4), scales=scales[:], in_=grouped[:].rearrange("p c j -> p (c j)")
            )
            return codes, scales

        offs_s = pick("offs_s", xs, U8, offs_t)
        two_s = pick("two_s", xs, U8, two_t)
        offs_w = pick("offs_w", xw, U32, offs_t)
        two_w = pick("two_w", xw, U32, two_t)
        wa_q = [quantize("wa_q%d" % i, cast_weight("wa_g%d" % i, raw)) for i, raw in enumerate(wa_raw)]
        wb_q = [quantize("wb_q%d" % i, cast_weight("wb_g%d" % i, raw)) for i, raw in enumerate(wb_raw)]

        def project(words, scales, weight_q, first_bank):
            banks = [bank(first_bank + t) for t in range(PACK)]
            for t in range(PACK):
                for (c0, c1), (codes, planes) in zip(W_CHUNKS, weight_q):
                    nc.tensor.matmul_mx(
                        out=banks[t][:, c0:c1],
                        lhsT=words[:, t, :].bitcast(FP8X4),
                        lhsT_scale=scales[:, t, :],
                        rhs=codes[:].bitcast(FP8X4),
                        rhs_scale=planes[:],
                        start=True,
                        stop=True,
                    )
            return banks

        y_ps = project(offs_w, offs_s, wa_q, PACK)
        d_ps = project(two_w, two_s, wb_q, 0)

        g2 = sb("g2", [P, PACK], F32)
        gh = sb("gh", [P, PACK], F32)
        nc.gpsimd.tensor_scalar(out=g2[:], in0=gt_t[:], scalar1=2.0, scalar2=0.0, op0=ALU.mult, op1=ALU.add)
        nc.gpsimd.tensor_scalar(out=gh[:], in0=gt_t[:], scalar1=-0.5, scalar2=0.0, op0=ALU.mult, op1=ALU.add)

        ntau2 = sb("ntau2", [P, PACK], F32)
        nc.gpsimd.tensor_scalar(out=ntau2[:], in0=tau2_t[:], scalar1=-1.0, scalar2=0.0, op0=ALU.mult, op1=ALU.add)
        top = sb("top", [P, PACK], F32)
        bias = sb("bias", [P, PACK], F32)
        ea = [h_sb[t][:, H : 2 * H] for t in range(PACK)]
        u = [h_sb[t][:, 2 * H : 3 * H] for t in range(PACK)]
        v = [h_sb[t][:, 3 * H : 4 * H] for t in range(PACK)]
        yg = [d_sb[t][:, H : 2 * H] for t in range(PACK)]
        zb = sb("zb", [P, PACK, H], BF16)

        for t in range(PACK):
            nc.vector.tensor_scalar(
                out=y_sb[t][:, 0:H], in0=y_ps[t][:], scalar1=g2[:, t : t + 1], scalar2=None, op0=ALU.mult
            )
            nc.scalar.activation(out=yg[t], in_=y_sb[t][:].indirect(n2_t[:]), func=ACT.Copy)
        for t in range(PACK):
            col = slice(t, t + 1)
            nc.vector.tensor_scalar(
                out=d_sb[t][:, 0:H], in0=d_ps[t][:], scalar1=1.0, scalar2=None, op0=ALU.mult, op1=ALU.max,
                accum_out=top[:, col],
            )
            nc.gpsimd.tensor_scalar(
                out=bias[:, col], in0=top[:, col], scalar1=tau_t[:, col], scalar2=-1.0, op0=ALU.mult, op1=ALU.mult
            )
        w1s_d = sb("w1s_d", [P, PACK, P], U8)
        nc.gpsimd.tensor_copy(out=w1s_d[:], in_=w1s[:].rearrange("p (m t) -> p t m", t=PACK))
        for t in range(PACK):
            nc.vector.tensor_tensor(out=u[t], in0=y_sb[t][:, 0:H], in1=yg[t], op=ALU.subtract)

        def exp_d(t, c0, c1):
            col = slice(t, t + 1)
            nc.scalar.activation(
                out=ea[t][:, c0:c1], in_=d_sb[t][:].indirect(n1_t[:, c0 // 16 : c1 // 16]), func=ACT.Exp,
                bias=bias[:, col], scale=tau_t[:, col],
            )

        def mix(t, c0, c1):
            nc.vector.tensor_tensor(out=v[t][:, c0:c1], in0=u[t][:, c0:c1], in1=ea[t][:, c0:c1], op=ALU.mult)
            nc.vector.scalar_tensor_tensor(
                out=zb[:, t, c0:c1], in0=d_sb[t][:, c0:c1], scalar=gh[:, t : t + 1], in1=v[t][:, c0:c1],
                op0=ALU.mult, op1=ALU.add,
            )

        for t in range(PACK - 1):
            exp_d(t, 0, H)
            mix(t, 0, H)
        for c0, c1 in Z_CHUNKS:
            exp_d(PACK - 1, c0, c1)
        w1w_d = keep.tile([P, PACK, P, 2], U8, name="w1w_d", tag="y_sb3", align_bytes=64)
        nc.scalar.copy(
            out=w1w_d[:].rearrange("p t m b -> p t (m b)").bitcast(U16),
            in_=w1w[:].bitcast(U16).rearrange("p (m t) -> p t m", t=PACK),
        )
        z_codes = sb("z_codes", [P, H], U32)
        z_scales = sb("z_scales", [P, H], U8)
        zi = []
        for ci, (c0, c1) in enumerate(Z_CHUNKS):
            mix(PACK - 1, c0, c1)
            grouped = sb("zi%d" % ci, [P, c1 - c0, PACK], BF16)
            dst, src = interleave_views(grouped, zb[:, :, c0:c1])
            if ci == 0:
                nc.scalar.copy(out=dst, in_=src)
            else:
                nc.vector.tensor_copy(out=dst, in_=src)
            zi.append(grouped)
        for (c0, c1), grouped in zip(Z_CHUNKS, zi):
            nc.vector.quantize_mx(
                out=z_codes[:, c0:c1].bitcast(FP8X4), scales=z_scales[:, c0:c1],
                in_=grouped[:].rearrange("p c j -> p (c j)"),
            )

        top2 = sb("top2", [P, PACK], F32)
        top2_part = sb("top2_part", [P, 1], F32)
        bias2 = [sb("bias2_%d" % t, [P, 1], F32) for t in range(PACK)]

        def mix_places(t, b, c0, c1, start_max, row_max):
            h_ps = bank(b)
            nc.tensor.matmul_mx(
                out=h_ps[:, 0 : c1 - c0],
                lhsT=w1w_d[:, t, :, :].rearrange("p m b -> p (m b)").bitcast(FP4X4),
                lhsT_scale=w1s_d[:, t, :],
                rhs=z_codes[:, c0:c1].bitcast(FP8X4),
                rhs_scale=z_scales[:, c0:c1],
                start=True,
                stop=True,
            )
            nc.vector.tensor_scalar(
                out=h_sb[t][:, c0:c1], in0=h_ps[:, 0 : c1 - c0], scalar1=1.0, scalar2=start_max, op0=ALU.mult,
                op1=ALU.max, accum_out=row_max,
            )

        mix_places(0, 0, 0, H // 2, None, top2_part[:])
        mix_places(0, PACK, H // 2, H, top2_part[:], top2[:, 0:1])
        nc.scalar.activation(out=bias2[0][:], in_=top2[:, 0:1], func=ACT.Copy, scale=ntau2[:, 0:1])
        for t in range(1, PACK):
            col = slice(t, t + 1)
            mix_places(t, PACK + t, 0, H, None, top2[:, col])
            nc.vector.tensor_tensor(out=bias2[t][:], in0=top2[:, col], in1=ntau2[:, col], op=ALU.mult)

        ms = sb("ms", [P, PACK, H], F32)
        hh = sb("hh", [P, PACK, H], F32)
        for t in range(PACK):
            col = slice(t, t + 1)
            for e0 in range(0, W, H_PIECE):
                e1 = e0 + H_PIECE
                ea2 = keep.tile([P, H_PIECE], F32, name="ea2", tag="ea2", bufs=3, align_bytes=64)
                nc.scalar.activation(
                    out=ea2[:], in_=h_sb[t][:].indirect(n3_t[:, e0 // 16 : e1 // 16]), func=ACT.Exp,
                    bias=bias2[t][:], scale=tau2_t[:, col],
                )
                nc.vector.tensor_reduce(
                    out=ms[:, t, e0 // 4 : e1 // 4], in_=ea2[:].rearrange("p (j r) -> p j r", r=4), axis=AX.X,
                    op=ALU.add,
                )
            nc.vector.tensor_scalar(
                out=hh[:, t, :], in0=h_sb[t][:, 0:H], scalar1=-0.5, scalar2=None, op0=ALU.mult
            )

        out_rows = out_0.rearrange("(p t) j -> p t j", t=PACK)
        out_words = out_1[0].rearrange("p c r -> p (c r)").bitcast(I32)
        o_codes = sb("o_codes", [P, H], U32)
        o_scales = sb("o_scales", [P, H], U8)
        rounding = []
        for group in O_GROUPS:
            g0, g1 = group[0][0], group[-1][1]
            o = sb("o%d" % g0, [P, PACK, g1 - g0], F32)
            for c0, c1 in group:
                lg = sb("lg%d" % c0, [P, PACK, c1 - c0], F32)
                nc.scalar.activation(out=lg[:], in_=ms[:, :, c0:c1], func=ACT.Ln, bias=quarter[:])
                nc.vector.tensor_tensor(out=o[:, :, c0 - g0 : c1 - g0], in0=lg[:], in1=hh[:, :, c0:c1], op=ALU.add)
                rounding.append((c0, c1, o[:, :, c0 - g0 : c1 - g0]))
            nc.sync.dma_start(out=out_rows[:, :, g0:g1], in_=o[:])
        for c0, c1, values in rounding:
            oi = sb("oi%d" % c0, [P, c1 - c0, PACK], BF16)
            dst, src = interleave_views(oi, values)
            if c0 in O_ON_SCALAR:
                nc.scalar.copy(out=dst, in_=src)
            else:
                nc.vector.tensor_copy(out=dst, in_=src)
            nc.vector.quantize_mx(
                out=o_codes[:, c0:c1].bitcast(FP8X4), scales=o_scales[:, c0:c1],
                in_=oi[:].rearrange("p c j -> p (c j)"),
            )
            if c1 == WORDS_SPLIT:
                nc.sync.dma_start(out=out_words[:, 0:c1], in_=o_codes[:, 0:c1].bitcast(I32))
        nc.sync.dma_start(out=out_words[:, WORDS_SPLIT:], in_=o_codes[:, WORDS_SPLIT:].bitcast(I32))
        for q in range(4):
            queue = nc.scalar if q % 2 == 0 else nc.sync
            queue.dma_start(
                out=out_2[0, 4 * q : 4 * q + 4, :].bitcast(I32), in_=o_scales[32 * q : 32 * q + 4, :].bitcast(I32)
            )
